import numpy as np
import ml_dtypes


def mxq(x, axis, fmt="e4m3"):
    dtype, down = {"e4m3": (ml_dtypes.float8_e4m3fn, 7), "e5m2": (ml_dtypes.float8_e5m2, 14)}[fmt]
    v = np.moveaxis(np.asarray(x, np.float32).astype(ml_dtypes.bfloat16).astype(np.float64), axis, -1)
    blocks = v.reshape(v.shape[:-1] + (-1, 32))
    amax = np.abs(blocks).max(-1, keepdims=True)
    byte = np.maximum(np.where(amax > 0, np.frexp(amax)[1] - 1 + 127, 0) - down, 1)
    scale = np.exp2(byte - 127.0)
    codes = (blocks / scale).astype(np.float32).astype(dtype).astype(np.float64)
    return np.moveaxis((codes * scale).reshape(v.shape), -1, axis)


WIDE = False


def mx_kscale(k):
    if not WIDE:
        return np.ones(k)
    levels = np.array([10, -10, 5, -5, 0])
    if k % 512:
        return np.exp2(np.random.permutation(np.resize(levels, k // 32))).repeat(32)
    a = np.empty((k // 512, 16))
    for p in range(k // 512):
        a[p, :8] = np.random.permutation(np.resize(levels, 8))
        for g in range(8):
            far = levels[np.abs(levels - a[p, g]) >= 10]
            a[p, g + 8] = far[np.random.randint(len(far))]
    return np.exp2(a.ravel()).repeat(32)


def f64(x):
    return np.asarray(x).astype(np.float64)


def striped(idx):
    return np.tile(idx.reshape(-1, 16).T, (8, 1)).astype(np.uint16)


def unstriped(offs):
    return offs[:16].T.reshape(-1).astype(np.int64)


def striped8(idx):
    return np.concatenate([x.reshape(-1, 16).T for x in idx]).astype(np.uint16)


def runs(offs, k):
    lists = np.stack([offs[16 * r : 16 * r + 16].T.reshape(-1) for r in range(8)]).astype(np.int64)
    return lists[np.arange(k) % 512 // 64]


def pack_weight(w):
    k, n = w.shape
    w = f64(np.asarray(w, np.float32).astype(ml_dtypes.bfloat16)).reshape(k // 32, 32, n)
    amax = np.abs(w).max(1)
    byte = np.clip(np.where(amax > 0, np.frexp(amax)[1] - 1 + 127 - 7, 1), 1, 254)
    scaled = (w * np.exp2(127.0 - byte)[:, None, :]).reshape(k, n).astype(np.float32)
    words = np.ascontiguousarray(scaled.reshape(k // 512, 128, 4, n).transpose(0, 1, 3, 2)).astype(ml_dtypes.float8_e4m3fn).view(np.uint8)
    return words, np.ascontiguousarray(byte.astype(np.uint8).reshape(k // 512, 16, n))


def unpack_weight(words, scales):
    g, p, n, _ = words.shape
    vals = np.ascontiguousarray(words).view(ml_dtypes.float8_e4m3fn).astype(np.float64) * np.repeat(np.exp2(scales.astype(np.float64) - 127.0), 8, axis=1)[..., None]
    return vals.transpose(0, 1, 3, 2).reshape(g * 512, n)


def sigmoid(v):
    return 1.0 / (1.0 + np.exp(-np.maximum(v, -700.0)))


K, T, S, H, C = 512, 2048, 512, 512, 512


def setup_inputs():
    n = np.random.standard_normal
    s = mx_kscale(K)[:, None]
    packed_xT = pack_weight(n((K, T)) * s)
    return {
        "x_words": packed_xT[0],
        "x_scales": packed_xT[1],
        "w1": (n((K, H)) / np.sqrt(K) / s).astype(np.float32),
        "sl": np.random.uniform(1.0, 2.0, (H, 1)).astype(np.float32),
        "th": (0.5 * n((H, 1))).astype(np.float32),
        "gs": (np.random.uniform(0.5, 1.5, (K, 1)) / s).astype(np.float32),
        "offs": striped(np.random.permutation(T)[:S]),
        "n1": striped(np.random.permutation(S)),
        "ca": striped(np.random.permutation(T)[:C]),
        "hc": striped8(np.random.randint(0, T, (8, C))),
        "n2": striped(np.random.permutation(S)),
        "n3": striped(np.random.permutation(S)),
    }


def reference(x_words, x_scales, w1, sl, th, gs, offs, n1, ca, hc, n2, n3):
    x_ca = unpack_weight(x_words, x_scales)[:, unstriped(ca)]
    xq = unpack_weight(x_words, x_scales)[:, unstriped(offs)]
    y = mxq(f64(w1), 0, "e4m3").T @ xq
    sg = sigmoid(f64(sl) * (y[:, unstriped(n1)] - f64(th)))
    z = f64(gs) * (y * sg)
    zq = mxq(z, 0, "e4m3")
    a = 0.0625 * (x_ca.T @ zq)
    x_hc = unpack_weight(x_words, x_scales)[np.arange(K)[:, None], runs(hc, K)]
    b = 0.0625 * (x_hc.T @ zq)
    return a + (sigmoid(b[:, unstriped(n3)] - b)) * (a[:, unstriped(n2)] - a)

@@ -1,0 +1,243 @@
+from contextlib import ExitStack
+
+import concourse.mybir as mybir
+
+K, T, S, H, C = 512, 2048, 512, 512, 512
+FLOPS = 2 * K * S * (H + 2 * C)
+
+F32 = mybir.dt.float32
+BF16 = mybir.dt.bfloat16
+I32 = mybir.dt.int32
+U32 = mybir.dt.uint32
+U16 = mybir.dt.uint16
+U8 = mybir.dt.uint8
+FP8X4 = mybir.dt.float8_e4m3fn_x4
+ALU = mybir.AluOpType
+ACT = mybir.ActivationFunctionType
+
+P = 128
+PACK = 4
+STRIPE = 16
+HALF = S // 2
+SIXTEENTH = 0.0625
+
+
+def tile_picked_cdhpullbesa_none_p_kernel(
+    tc, x_words, x_scales, w1, sl, th, gs, offs, n1, ca, hc, n2, n3, out
+):
+    nc = tc.nc
+    with ExitStack() as ctx:
+        keep = ctx.enter_context(tc.tile_pool(name="keep", bufs=1))
+        ring = ctx.enter_context(tc.tile_pool(name="ring", bufs=2))
+        psum = ctx.enter_context(tc.psum_pool(name="psum", bufs=1))
+
+        def load_list(source, name):
+            tile = keep.tile([P, S // STRIPE], U16, name=name)
+            nc.sync.dma_start(tile[:], source)
+            return tile
+
+        def entries(list_tile, first, count):
+            return list_tile[:, first // STRIPE : (first + count) // STRIPE]
+
+        def load_rows(queue, source, name):
+            tile = keep.tile([P, PACK], F32, name=name)
+            queue.dma_start(tile[:], source.rearrange("(p t) o -> p (t o)", t=PACK))
+            return tile
+
+        table_scales = keep.tile([P, T], U8, align_bytes=64)
+        nc.vector.memset(table_scales[:].bitcast(I32), 0)
+        offs_list = load_list(offs, "offs_list")
+        hc_list = load_list(hc, "hc_list")
+        ca_list = load_list(ca, "ca_list")
+        n1_list = load_list(n1, "n1_list")
+        n3_list = load_list(n3, "n3_list")
+        n2_list = load_list(n2, "n2_list")
+        table_words = keep.tile([P, T], U32, align_bytes=64)
+        nc.sync.dma_start(
+            table_words[:].bitcast(I32),
+            x_words[0].rearrange("p c r -> p (c r)").bitcast(I32),
+        )
+        w_rows = w1.rearrange("(p j) c -> p j c", j=PACK)
+
+        def load_w(h):
+            raw = keep.tile([P, PACK, H // 2], F32, name="w_raw", tag="w_raw%d" % h, align_bytes=64)
+            nc.sync.dma_start(raw[:], w_rows[:, :, h * (H // 2) : (h + 1) * (H // 2)])
+            return raw
+
+        w_raw = [load_w(0)]
+        scale_rows = x_scales[0].bitcast(I32)
+        scale_view = table_scales[:].bitcast(I32)
+        for r in range(2):
+            nc.sync.dma_start(scale_view[r:P:16, :], scale_rows[r:16:2, :])
+        for r in range(2, 4):
+            nc.sync.dma_start(scale_view[r:P:32, :], scale_rows[r:16:4, :])
+
+        w_raw.append(load_w(1))
+        slope = load_rows(nc.gpsimd, sl, "slope")
+        threshold = load_rows(nc.gpsimd, th, "threshold")
+        gain = load_rows(nc.gpsimd, gs, "gain")
+
+        def gather(table, list_tile, dtype, tag):
+            tile = keep.tile([P, S], dtype, name="picked", tag=tag, align_bytes=64)
+            nc.vector.tensor_copy(tile[:], table[:].indirect(list_tile[:]))
+            return tile
+
+        offs_words = gather(table_words, offs_list, U32, "offs_words")
+        hc_words = gather(table_words, hc_list, U32, "hc_words")
+        offs_scales = gather(table_scales, offs_list, U8, "offs_scales")
+
+        bias = keep.tile([P, PACK], F32)
+        nc.vector.scalar_tensor_tensor(bias[:], slope[:], -1.0, threshold[:], ALU.mult, ALU.mult)
+
+        w_grouped = keep.tile([P, PACK, P, PACK], BF16, tag="w_grouped", align_bytes=64)
+        w_walk = w_grouped[:].rearrange("p t m j -> p m j t")
+
+        def deal(engine_copy, h, m0, m1):
+            engine_copy(
+                w_walk[:, 64 * h + m0 : 64 * h + m1],
+                w_raw[h][:].rearrange("p j (m t) -> p m j t", t=PACK)[:, m0:m1],
+            )
+
+        deal(nc.scalar.copy, 0, 0, 64)
+        deal(nc.scalar.copy, 1, 0, 64)
+
+        banks = [psum.tile([P, S], F32, name="y_bank%d" % t, tag="bank%d" % t) for t in range(PACK)]
+        for t in range(PACK):
+            w_codes = keep.tile([P, P], U32, tag="w_codes%d" % t, align_bytes=64)
+            w_scales = keep.tile([P, P], U8, tag="w_scales%d" % t, align_bytes=64)
+            nc.vector.quantize_mx(
+                out=w_codes[:].bitcast(FP8X4),
+                scales=w_scales[:],
+                in_=w_grouped[:, t].rearrange("p m j -> p (m j)"),
+            )
+            nc.tensor.matmul_mx(
+                out=banks[t][:],
+                lhsT=w_codes[:].bitcast(FP8X4),
+                lhsT_scale=w_scales[:],
+                rhs=offs_words[:].bitcast(FP8X4),
+                rhs_scale=offs_scales[:],
+                start=True,
+                stop=True,
+            )
+
+        y = [keep.tile([P, S], F32, name="y%d" % t) for t in range(PACK)]
+        y_gained = keep.tile([P, PACK, S], F32)
+        gates = [keep.tile([P, PACK, HALF], F32, name="gates%d" % h) for h in range(2)]
+
+        def gate(t, h):
+            nc.scalar.activation(
+                gates[h][:, t, :],
+                y[t][:].indirect(entries(n1_list, h * HALF, HALF)),
+                ACT.Sigmoid,
+                bias=bias[:, t : t + 1],
+                scale=slope[:, t : t + 1],
+            )
+
+        for t in range(PACK):
+            if t != 0:
+                nc.scalar.copy(y[t][:], banks[t][:])
+            else:
+                nc.vector.tensor_copy(y[t][:], banks[t][:])
+            gate(t, 0)
+        hc_picked = gather(table_scales, hc_list, U8, "w_scales0")
+        hc_scales = keep.tile([P, C], U8, align_bytes=64)
+        nc.vector.tensor_copy(hc_scales[:].bitcast(I32), hc_picked[:].bitcast(I32))
+        for r in range(2):
+            nc.sync.dma_start(
+                hc_scales[:].bitcast(I32)[2 + r : P : 32, :],
+                hc_picked[:].bitcast(I32)[16 + r : P : 32, :],
+            )
+        ca_scales = gather(table_scales, ca_list, U8, "w_scales1")
+        ca_words = gather(table_words, ca_list, U32, "w_codes1")
+        for t in range(PACK):
+            nc.vector.tensor_scalar(y_gained[:, t, :], y[t][:], gain[:, t : t + 1], None, ALU.mult)
+        for t in range(PACK):
+            gate(t, 1)
+
+        z_codes = keep.tile([P, S], U32, align_bytes=64)
+        z_scales = keep.tile([P, S], U8, align_bytes=64)
+        for h in range(2):
+            cols = slice(h * HALF, (h + 1) * HALF)
+            z = keep.tile([P, HALF, PACK], BF16, name="z", tag="z", align_bytes=64)
+            nc.vector.tensor_tensor(
+                z[:].rearrange("p (c i) t -> p c t i", i=4),
+                y_gained[:, :, cols].rearrange("p t (c i) -> p c t i", i=4),
+                gates[h][:].rearrange("p t (c i) -> p c t i", i=4),
+                ALU.mult,
+            )
+            nc.vector.quantize_mx(
+                out=z_codes[:, cols].bitcast(FP8X4),
+                scales=z_scales[:, cols],
+                in_=z[:].rearrange("p j t -> p (j t)"),
+            )
+
+        def score(words, scales, r, bank):
+            rows = slice(r * P, (r + 1) * P)
+            sums = psum.tile([P, S], F32, name="sums", tag="bank%d" % bank)
+            for h in range(2):
+                cols = slice(h * HALF, (h + 1) * HALF)
+                nc.tensor.matmul_mx(
+                    out=sums[:, cols],
+                    lhsT=words[:, rows].bitcast(FP8X4),
+                    lhsT_scale=scales[:, rows],
+                    rhs=z_codes[:, cols].bitcast(FP8X4),
+                    rhs_scale=z_scales[:, cols],
+                    start=True,
+                    stop=True,
+                )
+            return sums
+
+        b_sums, a_sums = [], []
+        for r in range(C // P):
+            b_sums.append(score(hc_words, hc_scales, r, (2 * r + 4) % 8))
+            a_sums.append(score(ca_words, ca_scales, r, (2 * r + 5) % 8))
+
+        def fetch(window, list_tile, name, bufs):
+            far = ring.tile([P, S], F32, name=name, bufs=bufs)
+            for h in range(2):
+                nc.scalar.activation(
+                    far[:, h * HALF : (h + 1) * HALF],
+                    window[:].indirect(entries(list_tile, h * HALF, HALF)),
+                    ACT.Copy,
+                )
+            return far
+
+        blocks = C // P
+        pulls = []
+
+        def finish(r):
+            result = ring.tile([P, S], F32)
+            nc.vector.scalar_tensor_tensor(result[:], a_sums[r][:], SIXTEENTH, pulls[r][:], ALU.mult, ALU.add)
+            nc.sync.dma_start(out[r * P : (r + 1) * P, :], result[:])
+
+        def open_b(r):
+            window = ring.tile([P, S], F32, name="b_window", bufs=1)
+            nc.vector.tensor_copy(window[:], b_sums[r][:])
+            return window
+
+        def open_a(r):
+            window = ring.tile([P, S], F32, name="a_window", bufs=1)
+            nc.vector.tensor_scalar(window[:], a_sums[r][:], SIXTEENTH, None, ALU.mult)
+            return window
+
+        b_window, a_window = open_b(0), open_a(0)
+        for r in range(blocks):
+            last = r + 1 == blocks
+            b_step = fetch(b_window, n3_list, "b_step", 2)
+            a_far = fetch(a_window, n2_list, "a_far", 2)
+            nc.vector.tensor_tensor(b_step[:], b_step[:], b_sums[r][:], ALU.subtract)
+            share = ring.tile([P, S], F32)
+            nc.scalar.activation(share[:], b_step[:], ACT.Sigmoid, scale=SIXTEENTH)
+            if not last:
+                b_window = open_b(r + 1)
+            if r > 0:
+                finish(r - 1)
+            a_step = ring.tile([P, S], F32)
+            nc.vector.scalar_tensor_tensor(a_step[:], a_sums[r][:], -SIXTEENTH, a_far[:], ALU.mult, ALU.add)
+            if not last:
+                a_window = open_a(r + 1)
+            pull = ring.tile([P, S], F32)
+            engine = nc.vector if last else nc.gpsimd
+            engine.tensor_tensor(pull[:], a_step[:], share[:], ALU.mult)
+            pulls.append(pull)
+        finish(blocks - 1)

@@ -18,8 +18,13 @@ ACT = mybir.ActivationFunctionType
 P = 128
 PACK = 4
 STRIPE = 16
-HALF = S // 2
+QUADRANT = 32
+LINE = 4
+HALF = 256
+BLOCKS = C // P
 SIXTEENTH = 0.0625
+GROUPS = ((0, 256), (256, 128), (384, 128))
+HALVES = (slice(0, HALF), slice(HALF, 2 * HALF))
 
 
 def tile_picked_cdhpullbesa_none_p_kernel(
@@ -28,7 +33,7 @@ def tile_picked_cdhpullbesa_none_p_kernel(
     nc = tc.nc
     with ExitStack() as ctx:
         keep = ctx.enter_context(tc.tile_pool(name="keep", bufs=1))
-        ring = ctx.enter_context(tc.tile_pool(name="ring", bufs=2))
+        ring = ctx.enter_context(tc.tile_pool(name="ring", bufs=3))
         psum = ctx.enter_context(tc.psum_pool(name="psum", bufs=1))
 
         def load_list(source, name):
@@ -36,208 +41,247 @@ def tile_picked_cdhpullbesa_none_p_kernel(
             nc.sync.dma_start(tile[:], source)
             return tile
 
-        def entries(list_tile, first, count):
-            return list_tile[:, first // STRIPE : (first + count) // STRIPE]
+        def entries(list_tile, cols):
+            return list_tile[:, cols.start // STRIPE : cols.stop // STRIPE]
 
-        def load_rows(queue, source, name):
+        def load_per_row(queue, source, name):
             tile = keep.tile([P, PACK], F32, name=name)
             queue.dma_start(tile[:], source.rearrange("(p t) o -> p (t o)", t=PACK))
             return tile
 
+        def load_w(h):
+            tile = keep.tile([P, PACK * HALF], F32, name="w_raw%d" % h)
+            nc.sync.dma_start(
+                tile[:].rearrange("p (j c) -> p j c", j=PACK),
+                w1.rearrange("(p j) c -> p j c", j=PACK)[:, :, HALVES[h]],
+            )
+            return tile
+
         table_scales = keep.tile([P, T], U8, align_bytes=64)
         nc.vector.memset(table_scales[:].bitcast(I32), 0)
+
+        warm = keep.tile([P, 2], F32)
+        nc.vector.memset(warm[:, 0:1], 0.0)
+        nc.scalar.activation(warm[:, 1:2], warm[:, 0:1], ACT.Sigmoid)
+
         offs_list = load_list(offs, "offs_list")
         hc_list = load_list(hc, "hc_list")
         ca_list = load_list(ca, "ca_list")
         n1_list = load_list(n1, "n1_list")
         n3_list = load_list(n3, "n3_list")
         n2_list = load_list(n2, "n2_list")
+        slope = load_per_row(nc.sync, sl, "slope")
+        w_raw = [load_w(0)]
+
+        scale_rows = x_scales[0].bitcast(I32)
+        scale_view = table_scales[:].bitcast(I32)
+        for r in range(2):
+            nc.sync.dma_start(scale_view[r:P:STRIPE, :], scale_rows[r::2, :])
+        for r in range(2, 4):
+            nc.sync.dma_start(scale_view[r:P:QUADRANT, :], scale_rows[r::4, :])
+
+        w_raw.append(load_w(1))
         table_words = keep.tile([P, T], U32, align_bytes=64)
         nc.sync.dma_start(
             table_words[:].bitcast(I32),
             x_words[0].rearrange("p c r -> p (c r)").bitcast(I32),
         )
-        w_rows = w1.rearrange("(p j) c -> p j c", j=PACK)
+        threshold = load_per_row(nc.gpsimd, th, "threshold")
+        gain = load_per_row(nc.gpsimd, gs, "gain")
 
-        def load_w(h):
-            raw = keep.tile([P, PACK, H // 2], F32, name="w_raw", tag="w_raw%d" % h, align_bytes=64)
-            nc.sync.dma_start(raw[:], w_rows[:, :, h * (H // 2) : (h + 1) * (H // 2)])
-            return raw
+        shift = keep.tile([P, PACK], F32)
+        nc.gpsimd.tensor_tensor(shift[:], slope[:], threshold[:], ALU.mult)
+        bias = keep.tile([P, PACK], F32)
+        nc.gpsimd.tensor_scalar(bias[:], shift[:], -1.0, 0.0, ALU.mult, ALU.add)
 
-        w_raw = [load_w(0)]
-        scale_rows = x_scales[0].bitcast(I32)
-        scale_view = table_scales[:].bitcast(I32)
-        for r in range(2):
-            nc.sync.dma_start(scale_view[r:P:16, :], scale_rows[r:16:2, :])
-        for r in range(2, 4):
-            nc.sync.dma_start(scale_view[r:P:32, :], scale_rows[r:16:4, :])
-
-        w_raw.append(load_w(1))
-        slope = load_rows(nc.gpsimd, sl, "slope")
-        threshold = load_rows(nc.gpsimd, th, "threshold")
-        gain = load_rows(nc.gpsimd, gs, "gain")
-
-        def gather(table, list_tile, dtype, tag):
-            tile = keep.tile([P, S], dtype, name="picked", tag=tag, align_bytes=64)
-            nc.vector.tensor_copy(tile[:], table[:].indirect(list_tile[:]))
+        def pick(table, list_tile, cols, dtype, tag):
+            tile = keep.tile([P, cols.stop - cols.start], dtype, name="picked", tag=tag, align_bytes=64)
+            nc.vector.tensor_copy(tile[:], table[:].indirect(entries(list_tile, cols)))
             return tile
 
-        offs_words = gather(table_words, offs_list, U32, "offs_words")
-        hc_words = gather(table_words, hc_list, U32, "hc_words")
-        offs_scales = gather(table_scales, offs_list, U8, "offs_scales")
+        w_dealt = keep.tile([P, PACK, P, PACK], BF16, align_bytes=64)
 
-        bias = keep.tile([P, PACK], F32)
-        nc.vector.scalar_tensor_tensor(bias[:], slope[:], -1.0, threshold[:], ALU.mult, ALU.mult)
-
-        w_grouped = keep.tile([P, PACK, P, PACK], BF16, tag="w_grouped", align_bytes=64)
-        w_walk = w_grouped[:].rearrange("p t m j -> p m j t")
-
-        def deal(engine_copy, h, m0, m1):
-            engine_copy(
-                w_walk[:, 64 * h + m0 : 64 * h + m1],
-                w_raw[h][:].rearrange("p j (m t) -> p m j t", t=PACK)[:, m0:m1],
+        def deal_w(h):
+            m_count = HALF // PACK
+            nc.scalar.copy(
+                w_dealt[:].rearrange("p t m j -> p m j t")[:, h * m_count : (h + 1) * m_count],
+                w_raw[h][:].rearrange("p (j m t) -> p m j t", j=PACK, t=PACK),
             )
 
-        deal(nc.scalar.copy, 0, 0, 64)
-        deal(nc.scalar.copy, 1, 0, 64)
+        hc_scales = keep.tile([P, C], U8, align_bytes=64)
 
-        banks = [psum.tile([P, S], F32, name="y_bank%d" % t, tag="bank%d" % t) for t in range(PACK)]
+        def pick_hc_scales(h, tag):
+            picked = pick(table_scales, hc_list, HALVES[h], U8, tag)[:].bitcast(I32)
+            placed = hc_scales[:, HALVES[h]].bitcast(I32)
+            nc.vector.tensor_copy(placed, picked)
+            for r in range(2):
+                nc.sync.dma_start(placed[2 + r : P : QUADRANT, :], picked[STRIPE + r : P : QUADRANT, :])
+
+        def multiply(sums, stationary, stationary_scales, moving, moving_scales):
+            nc.tensor.matmul_mx(
+                out=sums,
+                lhsT=stationary.bitcast(FP8X4),
+                lhsT_scale=stationary_scales,
+                rhs=moving.bitcast(FP8X4),
+                rhs_scale=moving_scales,
+                start=True,
+                stop=True,
+            )
+
+        deal_w(0)
+        offs_scales = pick(table_scales, offs_list, slice(0, S), U8, "offs_scales")
+        deal_w(1)
+        pick_hc_scales(0, "hc_picked")
+        offs_words = [pick(table_words, offs_list, HALVES[h], U32, "offs_words%d" % h) for h in range(2)]
+
+        y_sums = [psum.tile([P, S], F32, name="y_sums", tag="bank%d" % t) for t in range(PACK)]
         for t in range(PACK):
             w_codes = keep.tile([P, P], U32, tag="w_codes%d" % t, align_bytes=64)
             w_scales = keep.tile([P, P], U8, tag="w_scales%d" % t, align_bytes=64)
             nc.vector.quantize_mx(
                 out=w_codes[:].bitcast(FP8X4),
                 scales=w_scales[:],
-                in_=w_grouped[:, t].rearrange("p m j -> p (m j)"),
+                in_=w_dealt[:, t].rearrange("p m j -> p (m j)"),
             )
-            nc.tensor.matmul_mx(
-                out=banks[t][:],
-                lhsT=w_codes[:].bitcast(FP8X4),
-                lhsT_scale=w_scales[:],
-                rhs=offs_words[:].bitcast(FP8X4),
-                rhs_scale=offs_scales[:],
-                start=True,
-                stop=True,
-            )
+            for h in range(2):
+                multiply(y_sums[t][:, HALVES[h]], w_codes[:], w_scales[:], offs_words[h][:], offs_scales[:, HALVES[h]])
 
         y = [keep.tile([P, S], F32, name="y%d" % t) for t in range(PACK)]
-        y_gained = keep.tile([P, PACK, S], F32)
-        gates = [keep.tile([P, PACK, HALF], F32, name="gates%d" % h) for h in range(2)]
+        y_gained = keep.tile([P, PACK * S], F32)
+        gates = [keep.tile([P, PACK * n], F32, name="gates%d" % g) for g, (first, n) in enumerate(GROUPS)]
 
-        def gate(t, h):
+        def gate(t, g):
+            first, n = GROUPS[g]
             nc.scalar.activation(
-                gates[h][:, t, :],
-                y[t][:].indirect(entries(n1_list, h * HALF, HALF)),
+                gates[g][:, t * n : (t + 1) * n],
+                y[t][:].indirect(entries(n1_list, slice(first, first + n))),
                 ACT.Sigmoid,
                 bias=bias[:, t : t + 1],
                 scale=slope[:, t : t + 1],
             )
 
+        hc_words = [pick(table_words, hc_list, HALVES[0], U32, "hc_words")]
         for t in range(PACK):
-            if t != 0:
-                nc.scalar.copy(y[t][:], banks[t][:])
+            if t == PACK - 1:
+                nc.scalar.copy(y[t][:], y_sums[t][:])
             else:
-                nc.vector.tensor_copy(y[t][:], banks[t][:])
+                nc.vector.tensor_copy(y[t][:], y_sums[t][:])
             gate(t, 0)
-        hc_picked = gather(table_scales, hc_list, U8, "w_scales0")
-        hc_scales = keep.tile([P, C], U8, align_bytes=64)
-        nc.vector.tensor_copy(hc_scales[:].bitcast(I32), hc_picked[:].bitcast(I32))
-        for r in range(2):
-            nc.sync.dma_start(
-                hc_scales[:].bitcast(I32)[2 + r : P : 32, :],
-                hc_picked[:].bitcast(I32)[16 + r : P : 32, :],
+        pick_hc_scales(1, "w_scales0")
+        hc_words.append(pick(table_words, hc_list, HALVES[1], U32, "w_codes0"))
+        for t in range(PACK):
+            nc.gpsimd.tensor_scalar(
+                y_gained[:, t * S : (t + 1) * S], y[t][:], gain[:, t : t + 1], 0.0, ALU.mult, ALU.add
             )
-        ca_scales = gather(table_scales, ca_list, U8, "w_scales1")
-        ca_words = gather(table_words, ca_list, U32, "w_codes1")
-        for t in range(PACK):
-            nc.vector.tensor_scalar(y_gained[:, t, :], y[t][:], gain[:, t : t + 1], None, ALU.mult)
-        for t in range(PACK):
-            gate(t, 1)
+        for g in range(1, len(GROUPS)):
+            for t in range(PACK):
+                gate(t, g)
 
         z_codes = keep.tile([P, S], U32, align_bytes=64)
         z_scales = keep.tile([P, S], U8, align_bytes=64)
-        for h in range(2):
-            cols = slice(h * HALF, (h + 1) * HALF)
-            z = keep.tile([P, HALF, PACK], BF16, name="z", tag="z", align_bytes=64)
+        for g, (first, n) in enumerate(GROUPS):
+            z = keep.tile([P, n, PACK], BF16, name="z", tag="z%d" % (g % 2), align_bytes=64)
             nc.vector.tensor_tensor(
-                z[:].rearrange("p (c i) t -> p c t i", i=4),
-                y_gained[:, :, cols].rearrange("p t (c i) -> p c t i", i=4),
-                gates[h][:].rearrange("p t (c i) -> p c t i", i=4),
+                z[:].rearrange("p (c i) t -> p c t i", i=LINE),
+                y_gained[:].rearrange("p (t c i) -> p c t i", t=PACK, i=LINE)[:, first // LINE : (first + n) // LINE],
+                gates[g][:].rearrange("p (t c i) -> p c t i", t=PACK, i=LINE),
                 ALU.mult,
             )
             nc.vector.quantize_mx(
-                out=z_codes[:, cols].bitcast(FP8X4),
-                scales=z_scales[:, cols],
+                out=z_codes[:, first : first + n].bitcast(FP8X4),
+                scales=z_scales[:, first : first + n],
                 in_=z[:].rearrange("p j t -> p (j t)"),
             )
 
+        ca_scales = pick(table_scales, ca_list, slice(0, C), U8, "w_scales1")
+        ca_words = [
+            pick(table_words, ca_list, HALVES[0], U32, "w_codes1"),
+            pick(table_words, ca_list, HALVES[1], U32, "z0"),
+        ]
+
         def score(words, scales, r, bank):
-            rows = slice(r * P, (r + 1) * P)
             sums = psum.tile([P, S], F32, name="sums", tag="bank%d" % bank)
-            for h in range(2):
-                cols = slice(h * HALF, (h + 1) * HALF)
-                nc.tensor.matmul_mx(
-                    out=sums[:, cols],
-                    lhsT=words[:, rows].bitcast(FP8X4),
-                    lhsT_scale=scales[:, rows],
-                    rhs=z_codes[:, cols].bitcast(FP8X4),
-                    rhs_scale=z_scales[:, cols],
-                    start=True,
-                    stop=True,
+            for first, n in GROUPS:
+                multiply(
+                    sums[:, first : first + n],
+                    words[r // 2][:, r % 2 * P : (r % 2 + 1) * P],
+                    scales[:, r * P : (r + 1) * P],
+                    z_codes[:, first : first + n],
+                    z_scales[:, first : first + n],
                 )
             return sums
 
-        b_sums, a_sums = [], []
-        for r in range(C // P):
-            b_sums.append(score(hc_words, hc_scales, r, (2 * r + 4) % 8))
-            a_sums.append(score(ca_words, ca_scales, r, (2 * r + 5) % 8))
+        b_sums = [score(hc_words, hc_scales, r, PACK + r) for r in range(BLOCKS)]
+        a_sums = [score(ca_words, ca_scales, r, r) for r in range(BLOCKS)]
 
-        def fetch(window, list_tile, name, bufs):
-            far = ring.tile([P, S], F32, name=name, bufs=bufs)
-            for h in range(2):
-                nc.scalar.activation(
-                    far[:, h * HALF : (h + 1) * HALF],
-                    window[:].indirect(entries(list_tile, h * HALF, HALF)),
-                    ACT.Copy,
-                )
-            return far
+        b_windows = [w_raw[r % 2] for r in range(BLOCKS)]
+        a_windows = [keep.tile([P, S], F32, name="a_window%d" % r) for r in range(BLOCKS)]
+        b_steps, a_steps, shares, pulls = [], [], [], []
 
-        blocks = C // P
-        pulls = []
+        def scale_out(window, sums, on_vector):
+            if on_vector:
+                nc.vector.tensor_scalar(window[:, :S], sums[:], SIXTEENTH, None, ALU.mult)
+            else:
+                nc.scalar.activation(window[:, :S], sums[:], ACT.Copy, scale=SIXTEENTH)
 
-        def finish(r):
-            result = ring.tile([P, S], F32)
-            nc.vector.scalar_tensor_tensor(result[:], a_sums[r][:], SIXTEENTH, pulls[r][:], ALU.mult, ALU.add)
-            nc.sync.dma_start(out[r * P : (r + 1) * P, :], result[:])
+        def fetch_b(r):
+            fetched = ring.tile([P, S], F32, name="b_step")
+            nc.scalar.activation(fetched[:], b_windows[r][:].indirect(n3_list[:]), ACT.Copy)
+            b_steps.append(fetched)
 
-        def open_b(r):
-            window = ring.tile([P, S], F32, name="b_window", bufs=1)
-            nc.vector.tensor_copy(window[:], b_sums[r][:])
-            return window
+        def fetch_a(r, on_vector):
+            fetched = ring.tile([P, S], F32, name="a_step")
+            for cols in HALVES:
+                looked_up = a_windows[r][:].indirect(entries(n2_list, cols))
+                if on_vector:
+                    nc.vector.tensor_copy(fetched[:, cols], looked_up)
+                else:
+                    nc.scalar.activation(fetched[:, cols], looked_up, ACT.Copy)
+            a_steps.append(fetched)
 
-        def open_a(r):
-            window = ring.tile([P, S], F32, name="a_window", bufs=1)
-            nc.vector.tensor_scalar(window[:], a_sums[r][:], SIXTEENTH, None, ALU.mult)
-            return window
+        def subtract_own(fetched, sums):
+            nc.vector.scalar_tensor_tensor(fetched[:], sums[:], -SIXTEENTH, fetched[:], ALU.mult, ALU.add)
 
-        b_window, a_window = open_b(0), open_a(0)
-        for r in range(blocks):
-            last = r + 1 == blocks
-            b_step = fetch(b_window, n3_list, "b_step", 2)
-            a_far = fetch(a_window, n2_list, "a_far", 2)
-            nc.vector.tensor_tensor(b_step[:], b_step[:], b_sums[r][:], ALU.subtract)
-            share = ring.tile([P, S], F32)
-            nc.scalar.activation(share[:], b_step[:], ACT.Sigmoid, scale=SIXTEENTH)
-            if not last:
-                b_window = open_b(r + 1)
+        def weigh(r):
+            share = ring.tile([P, S], F32, name="share")
+            nc.scalar.activation(share[:], b_steps[r][:], ACT.Sigmoid)
+            shares.append(share)
+            pulls.append(ring.tile([P, S], F32, name="pull"))
+
+        def pull(engine, r, cols):
+            engine.tensor_tensor(pulls[r][:, cols], a_steps[r][:, cols], shares[r][:, cols], ALU.mult)
+
+        def finish(r, cols):
+            result = ring.tile([P, cols.stop - cols.start], F32, name="result", bufs=BLOCKS + 1)
+            nc.vector.scalar_tensor_tensor(
+                result[:], a_sums[r][:, cols], SIXTEENTH, pulls[r][:, cols], ALU.mult, ALU.add
+            )
+            nc.sync.dma_start(out[r * P : (r + 1) * P, cols], result[:])
+
+        last = BLOCKS - 1
+        whole = slice(0, S)
+        scale_out(b_windows[0], b_sums[0], False)
+        scale_out(b_windows[1], b_sums[1], True)
+        fetch_b(0)
+        scale_out(a_windows[0], a_sums[0], True)
+        fetch_a(0, True)
+        for r in range(last):
+            nc.gpsimd.tensor_tensor(b_steps[r][:], b_steps[r][:], b_windows[r][:, :S], ALU.subtract)
+            fetch_b(r + 1)
+            scale_out(a_windows[r + 1], a_sums[r + 1], r + 1 < last)
+            weigh(r)
+            subtract_own(a_steps[r], a_sums[r])
+            pull(nc.gpsimd, r, whole)
+            if r + 2 < BLOCKS:
+                scale_out(b_windows[r + 2], b_sums[r + 2], False)
+            fetch_a(r + 1, r + 1 < last)
             if r > 0:
-                finish(r - 1)
-            a_step = ring.tile([P, S], F32)
-            nc.vector.scalar_tensor_tensor(a_step[:], a_sums[r][:], -SIXTEENTH, a_far[:], ALU.mult, ALU.add)
-            if not last:
-                a_window = open_a(r + 1)
-            pull = ring.tile([P, S], F32)
-            engine = nc.vector if last else nc.gpsimd
-            engine.tensor_tensor(pull[:], a_step[:], share[:], ALU.mult)
-            pulls.append(pull)
-        finish(blocks - 1)
+                finish(r - 1, whole)
+        subtract_own(b_steps[last], b_sums[last])
+        weigh(last)
+        subtract_own(a_steps[last], a_sums[last])
+        finish(last - 1, whole)
+        for cols in HALVES:
+            pull(nc.vector, last, cols)
+        for cols in HALVES:
+            finish(last, cols)

from contextlib import ExitStack

import concourse.mybir as mybir

K, T, S, H, C = 512, 2048, 512, 512, 512
FLOPS = 2 * K * S * (H + 2 * C)

F32 = mybir.dt.float32
BF16 = mybir.dt.bfloat16
I32 = mybir.dt.int32
U32 = mybir.dt.uint32
U16 = mybir.dt.uint16
U8 = mybir.dt.uint8
FP8X4 = mybir.dt.float8_e4m3fn_x4
ALU = mybir.AluOpType
ACT = mybir.ActivationFunctionType

P = 128
PACK = 4
STRIPE = 16
QUADRANT = 32
LINE = 4
HALF = 256
BLOCKS = C // P
SIXTEENTH = 0.0625
GROUPS = ((0, 256), (256, 128), (384, 128))
HALVES = (slice(0, HALF), slice(HALF, 2 * HALF))


def tile_picked_cdhpullbesa_none_p_kernel(
    tc, x_words, x_scales, w1, sl, th, gs, offs, n1, ca, hc, n2, n3, out
):
    nc = tc.nc
    with ExitStack() as ctx:
        keep = ctx.enter_context(tc.tile_pool(name="keep", bufs=1))
        ring = ctx.enter_context(tc.tile_pool(name="ring", bufs=3))
        psum = ctx.enter_context(tc.psum_pool(name="psum", bufs=1))

        def load_list(source, name):
            tile = keep.tile([P, S // STRIPE], U16, name=name)
            nc.sync.dma_start(tile[:], source)
            return tile

        def entries(list_tile, cols):
            return list_tile[:, cols.start // STRIPE : cols.stop // STRIPE]

        def load_per_row(queue, source, name):
            tile = keep.tile([P, PACK], F32, name=name)
            queue.dma_start(tile[:], source.rearrange("(p t) o -> p (t o)", t=PACK))
            return tile

        def load_w(h):
            tile = keep.tile([P, PACK * HALF], F32, name="w_raw%d" % h)
            nc.sync.dma_start(
                tile[:].rearrange("p (j c) -> p j c", j=PACK),
                w1.rearrange("(p j) c -> p j c", j=PACK)[:, :, HALVES[h]],
            )
            return tile

        table_scales = keep.tile([P, T], U8, align_bytes=64)
        nc.vector.memset(table_scales[:].bitcast(I32), 0)

        warm = keep.tile([P, 2], F32)
        nc.vector.memset(warm[:, 0:1], 0.0)
        nc.scalar.activation(warm[:, 1:2], warm[:, 0:1], ACT.Sigmoid)

        offs_list = load_list(offs, "offs_list")
        hc_list = load_list(hc, "hc_list")
        ca_list = load_list(ca, "ca_list")
        n1_list = load_list(n1, "n1_list")
        n3_list = load_list(n3, "n3_list")
        n2_list = load_list(n2, "n2_list")
        slope = load_per_row(nc.sync, sl, "slope")
        w_raw = [load_w(0)]

        scale_rows = x_scales[0].bitcast(I32)
        scale_view = table_scales[:].bitcast(I32)
        for r in range(2):
            nc.sync.dma_start(scale_view[r:P:STRIPE, :], scale_rows[r::2, :])
        for r in range(2, 4):
            nc.sync.dma_start(scale_view[r:P:QUADRANT, :], scale_rows[r::4, :])

        w_raw.append(load_w(1))
        table_words = keep.tile([P, T], U32, align_bytes=64)
        nc.sync.dma_start(
            table_words[:].bitcast(I32),
            x_words[0].rearrange("p c r -> p (c r)").bitcast(I32),
        )
        threshold = load_per_row(nc.gpsimd, th, "threshold")
        gain = load_per_row(nc.gpsimd, gs, "gain")

        shift = keep.tile([P, PACK], F32)
        nc.gpsimd.tensor_tensor(shift[:], slope[:], threshold[:], ALU.mult)
        bias = keep.tile([P, PACK], F32)
        nc.gpsimd.tensor_scalar(bias[:], shift[:], -1.0, 0.0, ALU.mult, ALU.add)

        def pick(table, list_tile, cols, dtype, tag):
            tile = keep.tile([P, cols.stop - cols.start], dtype, name="picked", tag=tag, align_bytes=64)
            nc.vector.tensor_copy(tile[:], table[:].indirect(entries(list_tile, cols)))
            return tile

        w_dealt = keep.tile([P, PACK, P, PACK], BF16, align_bytes=64)

        def deal_w(h):
            m_count = HALF // PACK
            nc.scalar.copy(
                w_dealt[:].rearrange("p t m j -> p m j t")[:, h * m_count : (h + 1) * m_count],
                w_raw[h][:].rearrange("p (j m t) -> p m j t", j=PACK, t=PACK),
            )

        hc_scales = keep.tile([P, C], U8, align_bytes=64)

        def pick_hc_scales(h, tag):
            picked = pick(table_scales, hc_list, HALVES[h], U8, tag)[:].bitcast(I32)
            placed = hc_scales[:, HALVES[h]].bitcast(I32)
            nc.vector.tensor_copy(placed, picked)
            for r in range(2):
                nc.sync.dma_start(placed[2 + r : P : QUADRANT, :], picked[STRIPE + r : P : QUADRANT, :])

        def multiply(sums, stationary, stationary_scales, moving, moving_scales):
            nc.tensor.matmul_mx(
                out=sums,
                lhsT=stationary.bitcast(FP8X4),
                lhsT_scale=stationary_scales,
                rhs=moving.bitcast(FP8X4),
                rhs_scale=moving_scales,
                start=True,
                stop=True,
            )

        deal_w(0)
        offs_scales = pick(table_scales, offs_list, slice(0, S), U8, "offs_scales")
        deal_w(1)
        pick_hc_scales(0, "hc_picked")
        offs_words = [pick(table_words, offs_list, HALVES[h], U32, "offs_words%d" % h) for h in range(2)]

        y_sums = [psum.tile([P, S], F32, name="y_sums", tag="bank%d" % t) for t in range(PACK)]
        for t in range(PACK):
            w_codes = keep.tile([P, P], U32, tag="w_codes%d" % t, align_bytes=64)
            w_scales = keep.tile([P, P], U8, tag="w_scales%d" % t, align_bytes=64)
            nc.vector.quantize_mx(
                out=w_codes[:].bitcast(FP8X4),
                scales=w_scales[:],
                in_=w_dealt[:, t].rearrange("p m j -> p (m j)"),
            )
            for h in range(2):
                multiply(y_sums[t][:, HALVES[h]], w_codes[:], w_scales[:], offs_words[h][:], offs_scales[:, HALVES[h]])

        y = [keep.tile([P, S], F32, name="y%d" % t) for t in range(PACK)]
        y_gained = keep.tile([P, PACK * S], F32)
        gates = [keep.tile([P, PACK * n], F32, name="gates%d" % g) for g, (first, n) in enumerate(GROUPS)]

        def gate(t, g):
            first, n = GROUPS[g]
            nc.scalar.activation(
                gates[g][:, t * n : (t + 1) * n],
                y[t][:].indirect(entries(n1_list, slice(first, first + n))),
                ACT.Sigmoid,
                bias=bias[:, t : t + 1],
                scale=slope[:, t : t + 1],
            )

        hc_words = [pick(table_words, hc_list, HALVES[0], U32, "hc_words")]
        for t in range(PACK):
            if t == PACK - 1:
                nc.scalar.copy(y[t][:], y_sums[t][:])
            else:
                nc.vector.tensor_copy(y[t][:], y_sums[t][:])
            gate(t, 0)
        pick_hc_scales(1, "w_scales0")
        hc_words.append(pick(table_words, hc_list, HALVES[1], U32, "w_codes0"))
        for t in range(PACK):
            nc.gpsimd.tensor_scalar(
                y_gained[:, t * S : (t + 1) * S], y[t][:], gain[:, t : t + 1], 0.0, ALU.mult, ALU.add
            )
        for g in range(1, len(GROUPS)):
            for t in range(PACK):
                gate(t, g)

        z_codes = keep.tile([P, S], U32, align_bytes=64)
        z_scales = keep.tile([P, S], U8, align_bytes=64)
        for g, (first, n) in enumerate(GROUPS):
            z = keep.tile([P, n, PACK], BF16, name="z", tag="z%d" % (g % 2), align_bytes=64)
            nc.vector.tensor_tensor(
                z[:].rearrange("p (c i) t -> p c t i", i=LINE),
                y_gained[:].rearrange("p (t c i) -> p c t i", t=PACK, i=LINE)[:, first // LINE : (first + n) // LINE],
                gates[g][:].rearrange("p (t c i) -> p c t i", t=PACK, i=LINE),
                ALU.mult,
            )
            nc.vector.quantize_mx(
                out=z_codes[:, first : first + n].bitcast(FP8X4),
                scales=z_scales[:, first : first + n],
                in_=z[:].rearrange("p j t -> p (j t)"),
            )

        ca_scales = pick(table_scales, ca_list, slice(0, C), U8, "w_scales1")
        ca_words = [
            pick(table_words, ca_list, HALVES[0], U32, "w_codes1"),
            pick(table_words, ca_list, HALVES[1], U32, "z0"),
        ]

        def score(words, scales, r, bank):
            sums = psum.tile([P, S], F32, name="sums", tag="bank%d" % bank)
            for first, n in GROUPS:
                multiply(
                    sums[:, first : first + n],
                    words[r // 2][:, r % 2 * P : (r % 2 + 1) * P],
                    scales[:, r * P : (r + 1) * P],
                    z_codes[:, first : first + n],
                    z_scales[:, first : first + n],
                )
            return sums

        b_sums = [score(hc_words, hc_scales, r, PACK + r) for r in range(BLOCKS)]
        a_sums = [score(ca_words, ca_scales, r, r) for r in range(BLOCKS)]

        b_windows = [w_raw[r % 2] for r in range(BLOCKS)]
        a_windows = [keep.tile([P, S], F32, name="a_window%d" % r) for r in range(BLOCKS)]
        b_steps, a_steps, shares, pulls = [], [], [], []

        def scale_out(window, sums, on_vector):
            if on_vector:
                nc.vector.tensor_scalar(window[:, :S], sums[:], SIXTEENTH, None, ALU.mult)
            else:
                nc.scalar.activation(window[:, :S], sums[:], ACT.Copy, scale=SIXTEENTH)

        def fetch_b(r):
            fetched = ring.tile([P, S], F32, name="b_step")
            nc.scalar.activation(fetched[:], b_windows[r][:].indirect(n3_list[:]), ACT.Copy)
            b_steps.append(fetched)

        def fetch_a(r, on_vector):
            fetched = ring.tile([P, S], F32, name="a_step")
            for cols in HALVES:
                looked_up = a_windows[r][:].indirect(entries(n2_list, cols))
                if on_vector:
                    nc.vector.tensor_copy(fetched[:, cols], looked_up)
                else:
                    nc.scalar.activation(fetched[:, cols], looked_up, ACT.Copy)
            a_steps.append(fetched)

        def subtract_own(fetched, sums):
            nc.vector.scalar_tensor_tensor(fetched[:], sums[:], -SIXTEENTH, fetched[:], ALU.mult, ALU.add)

        def weigh(r):
            share = ring.tile([P, S], F32, name="share")
            nc.scalar.activation(share[:], b_steps[r][:], ACT.Sigmoid)
            shares.append(share)
            pulls.append(ring.tile([P, S], F32, name="pull"))

        def pull(engine, r, cols):
            engine.tensor_tensor(pulls[r][:, cols], a_steps[r][:, cols], shares[r][:, cols], ALU.mult)

        def finish(r, cols):
            result = ring.tile([P, cols.stop - cols.start], F32, name="result", bufs=BLOCKS + 1)
            nc.vector.scalar_tensor_tensor(
                result[:], a_sums[r][:, cols], SIXTEENTH, pulls[r][:, cols], ALU.mult, ALU.add
            )
            nc.sync.dma_start(out[r * P : (r + 1) * P, cols], result[:])

        last = BLOCKS - 1
        whole = slice(0, S)
        scale_out(b_windows[0], b_sums[0], False)
        scale_out(b_windows[1], b_sums[1], True)
        fetch_b(0)
        scale_out(a_windows[0], a_sums[0], True)
        fetch_a(0, True)
        for r in range(last):
            nc.gpsimd.tensor_tensor(b_steps[r][:], b_steps[r][:], b_windows[r][:, :S], ALU.subtract)
            fetch_b(r + 1)
            scale_out(a_windows[r + 1], a_sums[r + 1], r + 1 < last)
            weigh(r)
            subtract_own(a_steps[r], a_sums[r])
            pull(nc.gpsimd, r, whole)
            if r + 2 < BLOCKS:
                scale_out(b_windows[r + 2], b_sums[r + 2], False)
            fetch_a(r + 1, r + 1 < last)
            if r > 0:
                finish(r - 1, whole)
        subtract_own(b_steps[last], b_sums[last])
        weigh(last)
        subtract_own(a_steps[last], a_sums[last])
        finish(last - 1, whole)
        for cols in HALVES:
            pull(nc.vector, last, cols)
        for cols in HALVES:
            finish(last, cols)
